import numpy as np
import ml_dtypes


def mxq(x, axis, fmt="e4m3"):
    dtype, down = {"e4m3": (ml_dtypes.float8_e4m3fn, 7), "e5m2": (ml_dtypes.float8_e5m2, 14)}[fmt]
    v = np.moveaxis(np.asarray(x, np.float32).astype(ml_dtypes.bfloat16).astype(np.float64), axis, -1)
    blocks = v.reshape(v.shape[:-1] + (-1, 32))
    amax = np.abs(blocks).max(-1, keepdims=True)
    byte = np.maximum(np.where(amax > 0, np.frexp(amax)[1] - 1 + 127, 0) - down, 1)
    scale = np.exp2(byte - 127.0)
    codes = (blocks / scale).astype(np.float32).astype(dtype).astype(np.float64)
    return np.moveaxis((codes * scale).reshape(v.shape), -1, axis)


WIDE = False


def mx_kscale(k):
    if not WIDE:
        return np.ones(k)
    levels = np.array([10, -10, 5, -5, 0])
    if k % 512:
        return np.exp2(np.random.permutation(np.resize(levels, k // 32))).repeat(32)
    a = np.empty((k // 512, 16))
    for p in range(k // 512):
        a[p, :8] = np.random.permutation(np.resize(levels, 8))
        for g in range(8):
            far = levels[np.abs(levels - a[p, g]) >= 10]
            a[p, g + 8] = far[np.random.randint(len(far))]
    return np.exp2(a.ravel()).repeat(32)


def f64(x):
    return np.asarray(x).astype(np.float64)


def striped(idx):
    return np.tile(idx.reshape(-1, 16).T, (8, 1)).astype(np.uint16)


def unstriped(offs):
    return offs[:16].T.reshape(-1).astype(np.int64)


def relu2(v):
    return np.maximum(v, 0.0) ** 2


K, T, S, N = 1024, 1024, 512, 256


def setup_inputs():
    n = np.random.standard_normal
    s = mx_kscale(K)[:, None]
    return {
        "xT": (n((K, T)) * s).astype(np.float32),
        "w": (n((K, N)) / np.sqrt(K) / s).astype(np.float32),
        "b": (0.3 * n((N, 1))).astype(np.float32),
        "gate": np.tile(np.random.uniform(0.2, 1.0, S), (N, 1)).astype(np.float32),
        "offs": striped(np.random.permutation(T)[:S]),
    }


def reference(xT, w, b, gate, offs):
    idx = unstriped(offs)
    xq = mxq(f64(xT)[:, idx], 0, "e4m3")
    y = mxq(f64(w), 0, "e4m3").T @ xq
    y = relu2(y + f64(b))
    out = np.zeros((N, T))
    out[:, idx] = f64(gate) * y
    return out

@@ -1,0 +1,147 @@
+from contextlib import ExitStack
+
+import concourse.mybir as mybir
+
+K, T, S, N = 1024, 1024, 512, 256
+FLOPS = 2 * K * S * N
+
+F32 = mybir.dt.float32
+BF16 = mybir.dt.bfloat16
+U32 = mybir.dt.uint32
+U16 = mybir.dt.uint16
+U8 = mybir.dt.uint8
+FP8X4 = mybir.dt.float8_e4m3fn_x4
+ACT = mybir.ActivationFunctionType
+MULT = mybir.AluOpType.mult
+
+P = 128
+PACK = 4
+K_PASS = P * PACK
+PASSES = K // K_PASS
+M_TILES = N // P
+GROUP = 16
+X_CHUNK = 512
+SCALAR_TOKENS = (512, 768, 768, 768)
+TAIL_SLICES = ((0, 128), (128, 256), (256, 512))
+
+
+def tile_picked_depth_lin_relu2_sub_e_kernel(tc, xT, w, b, gate, offs, out):
+    nc = tc.nc
+    with ExitStack() as ctx:
+        keep = ctx.enter_context(tc.tile_pool(name="keep", bufs=1))
+        psum = ctx.enter_context(tc.psum_pool(name="psum", bufs=1))
+
+        offsets = keep.tile([P, S // GROUP], U16, name="offsets")
+
+        def entries(lo, hi):
+            return offsets[:, lo // GROUP : hi // GROUP]
+
+        x_raw = {}
+        for a in range(PASSES):
+            rows = xT[a * K_PASS : (a + 1) * K_PASS, :].rearrange("(p j) t -> p j t", j=PACK)
+            for u in range(2):
+                for c in range(T // X_CHUNK):
+                    x_raw[a, u, c] = keep.tile([P, 2, X_CHUNK], F32, name=f"x_raw{a}{u}{c}", align_bytes=64)
+                    nc.sync.dma_start(x_raw[a, u, c][:], rows[:, 2 * u : 2 * u + 2, c * X_CHUNK : (c + 1) * X_CHUNK])
+                    if (a, u, c) == (0, 0, 1):
+                        nc.sync.dma_start(offsets[:], offs)
+        w_raw, gates, bias = {}, [], []
+        for m in range(M_TILES):
+            for a in range(PASSES):
+                rows = w[a * K_PASS : (a + 1) * K_PASS, :].rearrange("(p j) c -> p j c", j=PACK)
+                w_raw[m, a] = keep.tile([P, PACK, P], F32, name=f"w_raw{m}{a}", align_bytes=64)
+                nc.sync.dma_start(w_raw[m, a][:], rows[:, :, m * P : (m + 1) * P])
+            gates.append(keep.tile([P, S], F32, name=f"gate{m}", align_bytes=64))
+            nc.sync.dma_start(gates[m][:], gate[m * P : (m + 1) * P, :])
+            bias.append(keep.tile([P, 1], F32, name=f"bias{m}", align_bytes=64))
+            nc.scalar.dma_start(bias[m][:], b[m * P : (m + 1) * P, :])
+
+        windows = []
+        for m in range(M_TILES):
+            windows.append(keep.tile([P, T], F32, name=f"window{m}", align_bytes=64))
+            nc.vector.memset(windows[m][:], 0.0)
+        warm = keep.tile([P, 1], F32, name="warm", align_bytes=64)
+        nc.scalar.activation(warm[:], windows[0][:, 0:1], ACT.Relu)
+
+        x_codes = [keep.tile([P, S], U32, name=f"x_codes{a}", align_bytes=64) for a in range(PASSES)]
+        x_scales = [keep.tile([P, S], U8, name=f"x_scales{a}", align_bytes=64) for a in range(PASSES)]
+        picked = [keep.tile([P, S * PACK], BF16, name=f"picked{a}", align_bytes=64) for a in range(PASSES)]
+
+        def round_pairs(a, u):
+            pairs = keep.tile([P, T, 2], BF16, name=f"pairs{a}{u}", align_bytes=64)
+            split = SCALAR_TOKENS[2 * a + u]
+            cuts = sorted(set([0, X_CHUNK, split, T]))
+            for lo, hi in zip(cuts, cuts[1:]):
+                c = lo // X_CHUNK
+                src = x_raw[a, u, c][:, :, lo - c * X_CHUNK : hi - c * X_CHUNK].rearrange("p e t -> p t e")
+                if lo < split:
+                    nc.scalar.activation(pairs[:, lo:hi, :], src, ACT.Copy)
+                else:
+                    nc.vector.tensor_copy(pairs[:, lo:hi, :], src)
+            return pairs[:].rearrange("p t e -> p (t e)").bitcast(U32)
+
+        def gather(a, u, words, lo, hi):
+            dst = picked[a][:].bitcast(U32).rearrange("p (s u) -> p s u", u=2)
+            nc.vector.tensor_copy(dst[:, lo:hi, u], words.indirect(entries(lo, hi)))
+
+        def quantize_x(a, lo, hi):
+            nc.vector.quantize_mx(
+                out=x_codes[a][:, lo:hi].bitcast(FP8X4),
+                scales=x_scales[a][:, lo:hi],
+                in_=picked[a][:, lo * PACK : hi * PACK],
+            )
+
+        def quantize_w(m):
+            grouped = keep.tile([P, PASSES, P, PACK], BF16, name=f"w_grouped{m}", align_bytes=64)
+            for a in range(PASSES):
+                nc.scalar.activation(
+                    grouped[:, a].rearrange("p (c i) j -> p c j i", i=4),
+                    w_raw[m, a][:].rearrange("p j (c i) -> p c j i", i=4),
+                    ACT.Copy,
+                )
+            codes = keep.tile([P, PASSES * P], U32, name=f"w_codes{m}", align_bytes=64)
+            scales = keep.tile([P, PASSES * P], U8, name=f"w_scales{m}", align_bytes=64)
+            nc.vector.quantize_mx(
+                out=codes[:].bitcast(FP8X4),
+                scales=scales[:],
+                in_=grouped[:].rearrange("p a c j -> p (a c j)"),
+            )
+            return codes, scales
+
+        def layer(m, codes, scales, lo, hi):
+            acc = psum.tile([P, hi - lo], F32, name=f"acc{m}_{lo}")
+            for a in range(PASSES):
+                nc.tensor.matmul_mx(
+                    out=acc[:],
+                    lhsT=codes[:, a * P : (a + 1) * P].bitcast(FP8X4),
+                    lhsT_scale=scales[:, a * P : (a + 1) * P],
+                    rhs=x_codes[a][:, lo:hi].bitcast(FP8X4),
+                    rhs_scale=x_scales[a][:, lo:hi],
+                    start=(a == 0),
+                    stop=(a == PASSES - 1),
+                )
+            rectified = keep.tile([P, hi - lo], F32, name=f"rectified{m}_{lo}", align_bytes=64)
+            nc.scalar.activation(rectified[:], acc[:], ACT.Relu, bias=bias[m][:])
+            squared = keep.tile([P, hi - lo], F32, name=f"squared{m}_{lo}", align_bytes=64)
+            nc.scalar.activation(squared[:], rectified[:], ACT.Square)
+            return squared
+
+        def scatter(m, squared, lo, hi):
+            nc.vector.tensor_tensor(windows[m][:].indirect(entries(lo, hi)), squared[:], gates[m][:, lo:hi], MULT)
+
+        for a, u in ((0, 0), (0, 1), (1, 0)):
+            gather(a, u, round_pairs(a, u), 0, S)
+        quantize_x(0, 0, S)
+        last_words = round_pairs(1, 1)
+        for lo, hi in TAIL_SLICES:
+            gather(1, 1, last_words, lo, hi)
+        codes, scales = quantize_w(0)
+        for lo, hi in TAIL_SLICES:
+            quantize_x(1, lo, hi)
+        results = [layer(0, codes, scales, lo, hi) for lo, hi in TAIL_SLICES]
+        codes, scales = quantize_w(1)
+        for squared, (lo, hi) in zip(results, TAIL_SLICES):
+            scatter(0, squared, lo, hi)
+        nc.sync.dma_start(out[0:P, :], windows[0][:])
+        scatter(1, layer(1, codes, scales, 0, S), 0, S)
+        nc.sync.dma_start(out[P : 2 * P, :], windows[1][:])

@@ -20,9 +20,9 @@ K_PASS = P * PACK
 PASSES = K // K_PASS
 M_TILES = N // P
 GROUP = 16
-X_CHUNK = 512
-SCALAR_TOKENS = (512, 768, 768, 768)
-TAIL_SLICES = ((0, 128), (128, 256), (256, 512))
+LOAD_CUTS = ((0, 512, T), (0, 512, T), (0, 512, T), (0, 512, 768, T))
+SCALAR_TOKENS = ((864, T), (0, 512, 864, T), (0, 864), (0, 512))
+TAIL_SLICES = ((128, 256), (0, 128), (256, 512))
 
 
 def tile_picked_depth_lin_relu2_sub_e_kernel(tc, xT, w, b, gate, offs, out):
@@ -36,24 +36,40 @@ def tile_picked_depth_lin_relu2_sub_e_kernel(tc, xT, w, b, gate, offs, out):
         def entries(lo, hi):
             return offsets[:, lo // GROUP : hi // GROUP]
 
-        x_raw = {}
-        for a in range(PASSES):
+        x_raw, w_raw, gates, bias = {}, {}, {}, {}
+
+        def load_x(a, u, lo, hi):
             rows = xT[a * K_PASS : (a + 1) * K_PASS, :].rearrange("(p j) t -> p j t", j=PACK)
-            for u in range(2):
-                for c in range(T // X_CHUNK):
-                    x_raw[a, u, c] = keep.tile([P, 2, X_CHUNK], F32, name=f"x_raw{a}{u}{c}", align_bytes=64)
-                    nc.sync.dma_start(x_raw[a, u, c][:], rows[:, 2 * u : 2 * u + 2, c * X_CHUNK : (c + 1) * X_CHUNK])
-                    if (a, u, c) == (0, 0, 1):
-                        nc.sync.dma_start(offsets[:], offs)
-        w_raw, gates, bias = {}, [], []
-        for m in range(M_TILES):
-            for a in range(PASSES):
-                rows = w[a * K_PASS : (a + 1) * K_PASS, :].rearrange("(p j) c -> p j c", j=PACK)
-                w_raw[m, a] = keep.tile([P, PACK, P], F32, name=f"w_raw{m}{a}", align_bytes=64)
-                nc.sync.dma_start(w_raw[m, a][:], rows[:, :, m * P : (m + 1) * P])
-            gates.append(keep.tile([P, S], F32, name=f"gate{m}", align_bytes=64))
+            x_raw[a, u, lo] = keep.tile([P, 2, hi - lo], F32, name=f"x_raw{a}{u}_{lo}", align_bytes=64)
+            nc.sync.dma_start(x_raw[a, u, lo][:], rows[:, 2 * u : 2 * u + 2, lo:hi])
+
+        def load_w(a, lo, hi):
+            rows = w[a * K_PASS : (a + 1) * K_PASS, :].rearrange("(p j) c -> p j c", j=PACK)
+            raw = keep.tile([P, PACK, hi - lo], F32, name=f"w_raw{a}_{lo}", align_bytes=64)
+            nc.sync.dma_start(raw[:], rows[:, :, lo:hi])
+            for c in range(lo, hi, P):
+                w_raw[c // P, a] = raw[:, :, c - lo : c - lo + P]
+
+        def load_gate(m):
+            gates[m] = keep.tile([P, S], F32, name=f"gate{m}", align_bytes=64)
             nc.sync.dma_start(gates[m][:], gate[m * P : (m + 1) * P, :])
-            bias.append(keep.tile([P, 1], F32, name=f"bias{m}", align_bytes=64))
+
+        load_x(0, 0, 0, 512)
+        load_x(0, 0, 512, T)
+        nc.sync.dma_start(offsets[:], offs)
+        load_x(0, 1, 0, 512)
+        load_x(0, 1, 512, T)
+        load_x(1, 0, 0, 512)
+        load_x(1, 0, 512, T)
+        load_x(1, 1, 0, 512)
+        load_w(0, 0, N)
+        load_x(1, 1, 512, 768)
+        load_x(1, 1, 768, T)
+        load_w(1, 0, N)
+        load_gate(0)
+        load_gate(1)
+        for m in range(M_TILES):
+            bias[m] = keep.tile([P, 1], F32, name=f"bias{m}", align_bytes=64)
             nc.scalar.dma_start(bias[m][:], b[m * P : (m + 1) * P, :])
 
         windows = []
@@ -63,25 +79,29 @@ def tile_picked_depth_lin_relu2_sub_e_kernel(tc, xT, w, b, gate, offs, out):
         warm = keep.tile([P, 1], F32, name="warm", align_bytes=64)
         nc.scalar.activation(warm[:], windows[0][:, 0:1], ACT.Relu)
 
-        x_codes = [keep.tile([P, S], U32, name=f"x_codes{a}", align_bytes=64) for a in range(PASSES)]
-        x_scales = [keep.tile([P, S], U8, name=f"x_scales{a}", align_bytes=64) for a in range(PASSES)]
-        picked = [keep.tile([P, S * PACK], BF16, name=f"picked{a}", align_bytes=64) for a in range(PASSES)]
+        codes = [keep.tile([P, a * P + S], U32, name=f"codes{a}", align_bytes=64) for a in range(PASSES)]
+        scales = [keep.tile([P, a * P + S], U8, name=f"scales{a}", align_bytes=64) for a in range(PASSES)]
+        staged = [keep.tile([P, (a * P + S) * PACK], BF16, name=f"staged{a}", align_bytes=64) for a in range(PASSES)]
+        x_codes = [codes[a][:, a * P :] for a in range(PASSES)]
+        x_scales = [scales[a][:, a * P :] for a in range(PASSES)]
+        picked = [staged[a][:, a * P * PACK :] for a in range(PASSES)]
 
         def round_pairs(a, u):
             pairs = keep.tile([P, T, 2], BF16, name=f"pairs{a}{u}", align_bytes=64)
-            split = SCALAR_TOKENS[2 * a + u]
-            cuts = sorted(set([0, X_CHUNK, split, T]))
+            ranges = SCALAR_TOKENS[2 * a + u]
+            loads = LOAD_CUTS[2 * a + u]
+            cuts = sorted(set(loads + ranges))
             for lo, hi in zip(cuts, cuts[1:]):
-                c = lo // X_CHUNK
-                src = x_raw[a, u, c][:, :, lo - c * X_CHUNK : hi - c * X_CHUNK].rearrange("p e t -> p t e")
-                if lo < split:
+                first = max(c for c in loads if c <= lo)
+                src = x_raw[a, u, first][:, :, lo - first : hi - first].rearrange("p e t -> p t e")
+                if sum(1 for c in ranges if c <= lo) % 2:
                     nc.scalar.activation(pairs[:, lo:hi, :], src, ACT.Copy)
                 else:
                     nc.vector.tensor_copy(pairs[:, lo:hi, :], src)
             return pairs[:].rearrange("p t e -> p (t e)").bitcast(U32)
 
         def gather(a, u, words, lo, hi):
-            dst = picked[a][:].bitcast(U32).rearrange("p (s u) -> p s u", u=2)
+            dst = picked[a].bitcast(U32).rearrange("p (s u) -> p s u", u=2)
             nc.vector.tensor_copy(dst[:, lo:hi, u], words.indirect(entries(lo, hi)))
 
         def quantize_x(a, lo, hi):
@@ -91,30 +111,33 @@ def tile_picked_depth_lin_relu2_sub_e_kernel(tc, xT, w, b, gate, offs, out):
                 in_=picked[a][:, lo * PACK : hi * PACK],
             )
 
-        def quantize_w(m):
-            grouped = keep.tile([P, PASSES, P, PACK], BF16, name=f"w_grouped{m}", align_bytes=64)
-            for a in range(PASSES):
-                nc.scalar.activation(
-                    grouped[:, a].rearrange("p (c i) j -> p c j i", i=4),
-                    w_raw[m, a][:].rearrange("p j (c i) -> p c j i", i=4),
-                    ACT.Copy,
-                )
-            codes = keep.tile([P, PASSES * P], U32, name=f"w_codes{m}", align_bytes=64)
-            scales = keep.tile([P, PASSES * P], U8, name=f"w_scales{m}", align_bytes=64)
-            nc.vector.quantize_mx(
-                out=codes[:].bitcast(FP8X4),
-                scales=scales[:],
-                in_=grouped[:].rearrange("p a c j -> p (a c j)"),
-            )
-            return codes, scales
+        w_codes, w_scales = {}, {}
 
-        def layer(m, codes, scales, lo, hi):
+        def round_w(m, a, grouped):
+            nc.scalar.activation(
+                grouped.rearrange("p (c i j) -> p c j i", i=4, j=PACK),
+                w_raw[m, a].rearrange("p j (c i) -> p c j i", i=4),
+                ACT.Copy,
+            )
+
+        def quantize_w(m, a):
+            grouped = keep.tile([P, P * PACK], BF16, name=f"w_grouped{m}{a}", align_bytes=64)
+            round_w(m, a, grouped[:])
+            w_codes[m, a] = keep.tile([P, P], U32, name=f"w_codes{m}{a}", align_bytes=64)
+            w_scales[m, a] = keep.tile([P, P], U8, name=f"w_scales{m}{a}", align_bytes=64)
+            nc.vector.quantize_mx(
+                out=w_codes[m, a][:].bitcast(FP8X4),
+                scales=w_scales[m, a][:],
+                in_=grouped[:],
+            )
+
+        def layer(m, lo, hi):
             acc = psum.tile([P, hi - lo], F32, name=f"acc{m}_{lo}")
             for a in range(PASSES):
                 nc.tensor.matmul_mx(
                     out=acc[:],
-                    lhsT=codes[:, a * P : (a + 1) * P].bitcast(FP8X4),
-                    lhsT_scale=scales[:, a * P : (a + 1) * P],
+                    lhsT=w_codes[m, a][:, :].bitcast(FP8X4),
+                    lhsT_scale=w_scales[m, a][:, :],
                     rhs=x_codes[a][:, lo:hi].bitcast(FP8X4),
                     rhs_scale=x_scales[a][:, lo:hi],
                     start=(a == 0),
@@ -129,19 +152,31 @@ def tile_picked_depth_lin_relu2_sub_e_kernel(tc, xT, w, b, gate, offs, out):
         def scatter(m, squared, lo, hi):
             nc.vector.tensor_tensor(windows[m][:].indirect(entries(lo, hi)), squared[:], gates[m][:, lo:hi], MULT)
 
-        for a, u in ((0, 0), (0, 1), (1, 0)):
-            gather(a, u, round_pairs(a, u), 0, S)
+        gather(0, 0, round_pairs(0, 0), 0, S)
+        gather(0, 1, round_pairs(0, 1), 0, S)
+        words = round_pairs(1, 0)
         quantize_x(0, 0, S)
-        last_words = round_pairs(1, 1)
+        gather(1, 0, words, 0, S)
+        words = round_pairs(1, 1)
+        quantize_w(0, 0)
+        quantize_w(1, 0)
+        first, second, third = TAIL_SLICES
+        gather(1, 1, words, *first)
+        gather(1, 1, words, *second)
+        quantize_x(1, *first)
+        quantize_w(0, 1)
+        gather(1, 1, words, 256, 384)
+        round_w(1, 1, staged[1][:, : P * PACK])
+        gather(1, 1, words, 384, 512)
+        nc.vector.quantize_mx(
+            out=codes[1][:, : 2 * P].bitcast(FP8X4),
+            scales=scales[1][:, : 2 * P],
+            in_=staged[1][:, : 2 * P * PACK],
+        )
+        w_codes[1, 1], w_scales[1, 1] = codes[1][:, :P], scales[1][:, :P]
+        quantize_x(1, *third)
         for lo, hi in TAIL_SLICES:
-            gather(1, 1, last_words, lo, hi)
-        codes, scales = quantize_w(0)
-        for lo, hi in TAIL_SLICES:
-            quantize_x(1, lo, hi)
-        results = [layer(0, codes, scales, lo, hi) for lo, hi in TAIL_SLICES]
-        codes, scales = quantize_w(1)
-        for squared, (lo, hi) in zip(results, TAIL_SLICES):
-            scatter(0, squared, lo, hi)
-        nc.sync.dma_start(out[0:P, :], windows[0][:])
-        scatter(1, layer(1, codes, scales, 0, S), 0, S)
-        nc.sync.dma_start(out[P : 2 * P, :], windows[1][:])
+            for m in range(M_TILES):
+                scatter(m, layer(m, lo, hi), lo, hi)
+        for m in range(M_TILES):
+            nc.sync.dma_start(out[m * P : (m + 1) * P, :], windows[m][:])

@@ -8,6 +8,7 @@ FLOPS = 2 * K * S * N
 F32 = mybir.dt.float32
 BF16 = mybir.dt.bfloat16
 U32 = mybir.dt.uint32
+I32 = mybir.dt.int32
 U16 = mybir.dt.uint16
 U8 = mybir.dt.uint8
 FP8X4 = mybir.dt.float8_e4m3fn_x4
@@ -100,9 +101,15 @@ def tile_picked_depth_lin_relu2_sub_e_kernel(tc, xT, w, b, gate, offs, out):
                     nc.vector.tensor_copy(pairs[:, lo:hi, :], src)
             return pairs[:].rearrange("p t e -> p (t e)").bitcast(U32)
 
+        gathered = [keep.tile([P, 2, S], U32, name=f"gathered{a}", align_bytes=64) for a in range(PASSES)]
+
         def gather(a, u, words, lo, hi):
-            dst = picked[a].bitcast(U32).rearrange("p (s u) -> p s u", u=2)
-            nc.vector.tensor_copy(dst[:, lo:hi, u], words.indirect(entries(lo, hi)))
+            nc.vector.tensor_copy(gathered[a][:, u, lo:hi], words.indirect(entries(lo, hi)))
+
+        def interleave(a, lo, hi):
+            dst = picked[a].bitcast(I32).rearrange("p (s u) -> p s u", u=2)
+            src = gathered[a][:].bitcast(I32).rearrange("p u s -> p s u")
+            nc.vector.tensor_copy(dst[:, lo:hi, :], src[:, lo:hi, :])
 
         def quantize_x(a, lo, hi):
             nc.vector.quantize_mx(
@@ -155,6 +162,7 @@ def tile_picked_depth_lin_relu2_sub_e_kernel(tc, xT, w, b, gate, offs, out):
         gather(0, 0, round_pairs(0, 0), 0, S)
         gather(0, 1, round_pairs(0, 1), 0, S)
         words = round_pairs(1, 0)
+        interleave(0, 0, S)
         quantize_x(0, 0, S)
         gather(1, 0, words, 0, S)
         words = round_pairs(1, 1)
@@ -162,9 +170,11 @@ def tile_picked_depth_lin_relu2_sub_e_kernel(tc, xT, w, b, gate, offs, out):
         quantize_w(1, 0)
         first, second, third = TAIL_SLICES
         gather(1, 1, words, *first)
+        interleave(1, *first)
         gather(1, 1, words, *second)
         quantize_x(1, *first)
         quantize_w(0, 1)
+        interleave(1, *second)
         gather(1, 1, words, 256, 384)
         round_w(1, 1, staged[1][:, : P * PACK])
         gather(1, 1, words, 384, 512)
@@ -174,6 +184,7 @@ def tile_picked_depth_lin_relu2_sub_e_kernel(tc, xT, w, b, gate, offs, out):
             in_=staged[1][:, : 2 * P * PACK],
         )
         w_codes[1, 1], w_scales[1, 1] = codes[1][:, :P], scales[1][:, :P]
+        interleave(1, *third)
         quantize_x(1, *third)
         for lo, hi in TAIL_SLICES:
             for m in range(M_TILES):

from contextlib import ExitStack

import concourse.mybir as mybir

K, T, S, N = 1024, 1024, 512, 256
FLOPS = 2 * K * S * N

F32 = mybir.dt.float32
BF16 = mybir.dt.bfloat16
U32 = mybir.dt.uint32
I32 = mybir.dt.int32
U16 = mybir.dt.uint16
U8 = mybir.dt.uint8
FP8X4 = mybir.dt.float8_e4m3fn_x4
ACT = mybir.ActivationFunctionType
MULT = mybir.AluOpType.mult

P = 128
PACK = 4
K_PASS = P * PACK
PASSES = K // K_PASS
M_TILES = N // P
GROUP = 16
LOAD_CUTS = ((0, 512, T), (0, 512, T), (0, 512, T), (0, 512, 768, T))
SCALAR_TOKENS = ((864, T), (0, 512, 864, T), (0, 864), (0, 512))
TAIL_SLICES = ((128, 256), (0, 128), (256, 512))


def tile_picked_depth_lin_relu2_sub_e_kernel(tc, xT, w, b, gate, offs, out):
    nc = tc.nc
    with ExitStack() as ctx:
        keep = ctx.enter_context(tc.tile_pool(name="keep", bufs=1))
        psum = ctx.enter_context(tc.psum_pool(name="psum", bufs=1))

        offsets = keep.tile([P, S // GROUP], U16, name="offsets")

        def entries(lo, hi):
            return offsets[:, lo // GROUP : hi // GROUP]

        x_raw, w_raw, gates, bias = {}, {}, {}, {}

        def load_x(a, u, lo, hi):
            rows = xT[a * K_PASS : (a + 1) * K_PASS, :].rearrange("(p j) t -> p j t", j=PACK)
            x_raw[a, u, lo] = keep.tile([P, 2, hi - lo], F32, name=f"x_raw{a}{u}_{lo}", align_bytes=64)
            nc.sync.dma_start(x_raw[a, u, lo][:], rows[:, 2 * u : 2 * u + 2, lo:hi])

        def load_w(a, lo, hi):
            rows = w[a * K_PASS : (a + 1) * K_PASS, :].rearrange("(p j) c -> p j c", j=PACK)
            raw = keep.tile([P, PACK, hi - lo], F32, name=f"w_raw{a}_{lo}", align_bytes=64)
            nc.sync.dma_start(raw[:], rows[:, :, lo:hi])
            for c in range(lo, hi, P):
                w_raw[c // P, a] = raw[:, :, c - lo : c - lo + P]

        def load_gate(m):
            gates[m] = keep.tile([P, S], F32, name=f"gate{m}", align_bytes=64)
            nc.sync.dma_start(gates[m][:], gate[m * P : (m + 1) * P, :])

        load_x(0, 0, 0, 512)
        load_x(0, 0, 512, T)
        nc.sync.dma_start(offsets[:], offs)
        load_x(0, 1, 0, 512)
        load_x(0, 1, 512, T)
        load_x(1, 0, 0, 512)
        load_x(1, 0, 512, T)
        load_x(1, 1, 0, 512)
        load_w(0, 0, N)
        load_x(1, 1, 512, 768)
        load_x(1, 1, 768, T)
        load_w(1, 0, N)
        load_gate(0)
        load_gate(1)
        for m in range(M_TILES):
            bias[m] = keep.tile([P, 1], F32, name=f"bias{m}", align_bytes=64)
            nc.scalar.dma_start(bias[m][:], b[m * P : (m + 1) * P, :])

        windows = []
        for m in range(M_TILES):
            windows.append(keep.tile([P, T], F32, name=f"window{m}", align_bytes=64))
            nc.vector.memset(windows[m][:], 0.0)
        warm = keep.tile([P, 1], F32, name="warm", align_bytes=64)
        nc.scalar.activation(warm[:], windows[0][:, 0:1], ACT.Relu)

        codes = [keep.tile([P, a * P + S], U32, name=f"codes{a}", align_bytes=64) for a in range(PASSES)]
        scales = [keep.tile([P, a * P + S], U8, name=f"scales{a}", align_bytes=64) for a in range(PASSES)]
        staged = [keep.tile([P, (a * P + S) * PACK], BF16, name=f"staged{a}", align_bytes=64) for a in range(PASSES)]
        x_codes = [codes[a][:, a * P :] for a in range(PASSES)]
        x_scales = [scales[a][:, a * P :] for a in range(PASSES)]
        picked = [staged[a][:, a * P * PACK :] for a in range(PASSES)]

        def round_pairs(a, u):
            pairs = keep.tile([P, T, 2], BF16, name=f"pairs{a}{u}", align_bytes=64)
            ranges = SCALAR_TOKENS[2 * a + u]
            loads = LOAD_CUTS[2 * a + u]
            cuts = sorted(set(loads + ranges))
            for lo, hi in zip(cuts, cuts[1:]):
                first = max(c for c in loads if c <= lo)
                src = x_raw[a, u, first][:, :, lo - first : hi - first].rearrange("p e t -> p t e")
                if sum(1 for c in ranges if c <= lo) % 2:
                    nc.scalar.activation(pairs[:, lo:hi, :], src, ACT.Copy)
                else:
                    nc.vector.tensor_copy(pairs[:, lo:hi, :], src)
            return pairs[:].rearrange("p t e -> p (t e)").bitcast(U32)

        gathered = [keep.tile([P, 2, S], U32, name=f"gathered{a}", align_bytes=64) for a in range(PASSES)]

        def gather(a, u, words, lo, hi):
            nc.vector.tensor_copy(gathered[a][:, u, lo:hi], words.indirect(entries(lo, hi)))

        def interleave(a, lo, hi):
            dst = picked[a].bitcast(I32).rearrange("p (s u) -> p s u", u=2)
            src = gathered[a][:].bitcast(I32).rearrange("p u s -> p s u")
            nc.vector.tensor_copy(dst[:, lo:hi, :], src[:, lo:hi, :])

        def quantize_x(a, lo, hi):
            nc.vector.quantize_mx(
                out=x_codes[a][:, lo:hi].bitcast(FP8X4),
                scales=x_scales[a][:, lo:hi],
                in_=picked[a][:, lo * PACK : hi * PACK],
            )

        w_codes, w_scales = {}, {}

        def round_w(m, a, grouped):
            nc.scalar.activation(
                grouped.rearrange("p (c i j) -> p c j i", i=4, j=PACK),
                w_raw[m, a].rearrange("p j (c i) -> p c j i", i=4),
                ACT.Copy,
            )

        def quantize_w(m, a):
            grouped = keep.tile([P, P * PACK], BF16, name=f"w_grouped{m}{a}", align_bytes=64)
            round_w(m, a, grouped[:])
            w_codes[m, a] = keep.tile([P, P], U32, name=f"w_codes{m}{a}", align_bytes=64)
            w_scales[m, a] = keep.tile([P, P], U8, name=f"w_scales{m}{a}", align_bytes=64)
            nc.vector.quantize_mx(
                out=w_codes[m, a][:].bitcast(FP8X4),
                scales=w_scales[m, a][:],
                in_=grouped[:],
            )

        def layer(m, lo, hi):
            acc = psum.tile([P, hi - lo], F32, name=f"acc{m}_{lo}")
            for a in range(PASSES):
                nc.tensor.matmul_mx(
                    out=acc[:],
                    lhsT=w_codes[m, a][:, :].bitcast(FP8X4),
                    lhsT_scale=w_scales[m, a][:, :],
                    rhs=x_codes[a][:, lo:hi].bitcast(FP8X4),
                    rhs_scale=x_scales[a][:, lo:hi],
                    start=(a == 0),
                    stop=(a == PASSES - 1),
                )
            rectified = keep.tile([P, hi - lo], F32, name=f"rectified{m}_{lo}", align_bytes=64)
            nc.scalar.activation(rectified[:], acc[:], ACT.Relu, bias=bias[m][:])
            squared = keep.tile([P, hi - lo], F32, name=f"squared{m}_{lo}", align_bytes=64)
            nc.scalar.activation(squared[:], rectified[:], ACT.Square)
            return squared

        def scatter(m, squared, lo, hi):
            nc.vector.tensor_tensor(windows[m][:].indirect(entries(lo, hi)), squared[:], gates[m][:, lo:hi], MULT)

        gather(0, 0, round_pairs(0, 0), 0, S)
        gather(0, 1, round_pairs(0, 1), 0, S)
        words = round_pairs(1, 0)
        interleave(0, 0, S)
        quantize_x(0, 0, S)
        gather(1, 0, words, 0, S)
        words = round_pairs(1, 1)
        quantize_w(0, 0)
        quantize_w(1, 0)
        first, second, third = TAIL_SLICES
        gather(1, 1, words, *first)
        interleave(1, *first)
        gather(1, 1, words, *second)
        quantize_x(1, *first)
        quantize_w(0, 1)
        interleave(1, *second)
        gather(1, 1, words, 256, 384)
        round_w(1, 1, staged[1][:, : P * PACK])
        gather(1, 1, words, 384, 512)
        nc.vector.quantize_mx(
            out=codes[1][:, : 2 * P].bitcast(FP8X4),
            scales=scales[1][:, : 2 * P],
            in_=staged[1][:, : 2 * P * PACK],
        )
        w_codes[1, 1], w_scales[1, 1] = codes[1][:, :P], scales[1][:, :P]
        interleave(1, *third)
        quantize_x(1, *third)
        for lo, hi in TAIL_SLICES:
            for m in range(M_TILES):
                scatter(m, layer(m, lo, hi), lo, hi)
        for m in range(M_TILES):
            nc.sync.dma_start(out[m * P : (m + 1) * P, :], windows[m][:])
